import numpy as np
import ml_dtypes


def mxq(x, axis, fmt="e4m3"):
    dtype, down = {"e4m3": (ml_dtypes.float8_e4m3fn, 7), "e5m2": (ml_dtypes.float8_e5m2, 14)}[fmt]
    v = np.moveaxis(np.asarray(x, np.float32).astype(ml_dtypes.bfloat16).astype(np.float64), axis, -1)
    blocks = v.reshape(v.shape[:-1] + (-1, 32))
    amax = np.abs(blocks).max(-1, keepdims=True)
    byte = np.maximum(np.where(amax > 0, np.frexp(amax)[1] - 1 + 127, 0) - down, 1)
    scale = np.exp2(byte - 127.0)
    codes = (blocks / scale).astype(np.float32).astype(dtype).astype(np.float64)
    return np.moveaxis((codes * scale).reshape(v.shape), -1, axis)


WIDE = False


def mx_kscale(k, group=512):
    if not WIDE:
        return np.ones(k)
    levels = np.array([18, -18])
    if group != 512:
        return np.exp2(np.random.permutation(np.resize(levels, k // group))).repeat(group)
    if k % 512:
        return np.exp2(np.random.permutation(np.resize(levels, k // 32))).repeat(32)
    a = np.empty((k // 512, 16))
    for p in range(k // 512):
        a[p, :8] = np.random.permutation(np.resize(levels, 8))
        for g in range(8):
            far = levels[np.abs(levels - a[p, g]) >= 10]
            a[p, g + 8] = far[np.random.randint(len(far))]
    return np.exp2(a.ravel()).repeat(32)


def f64(x):
    return np.asarray(x).astype(np.float64)


H, D, N = 4, 128, 512


def setup_inputs():
    n = np.random.standard_normal
    s = mx_kscale(D, 0)
    u = mx_kscale(N)
    t = np.random.uniform(0.5, 2.0, N) * u
    v = n((H, N, 128))
    return {
        "q": n((H, D, N)).astype(np.float32),
        "qa": (np.random.uniform(0.5, 2.0, D) * s)[:, None].astype(np.float32),
        "ka": np.tile(np.random.uniform(0.5, 2.0, D) / s, (128, 1)).astype(np.float32),
        "k": n((H, N, D)).astype(np.float32),
        "t": t.reshape(N, 1).astype(np.float32),
        "v": (v / t[:, None]).astype(np.float32),
        "og": n((H, N, 128)).astype(np.float32),
    }


def reference(q, qa, ka, k, t, v, og):
    fq = (np.maximum(f64(q), 0.0) + 0.125) * f64(qa)
    fk = (np.maximum(f64(k), 0.0) + 0.125) * f64(t) * f64(ka)[:1]
    S = (mxq(fk, 1, "e4m3").transpose(0, 2, 1) @ mxq(f64(v), 1, "e4m3")) / N
    y = mxq(fq, 1, "e4m3").transpose(0, 2, 1) @ mxq(S, 1, "e4m3")
    y = y / (1.0 + np.exp(-f64(og)))
    return y

@@ -1,0 +1,295 @@
+from contextlib import ExitStack
+
+import concourse.mybir as mybir
+
+H, D, N = 4, 128, 512
+FLOPS = 2 * 2 * H * N * D * D
+
+F32 = mybir.dt.float32
+BF16 = mybir.dt.bfloat16
+I32 = mybir.dt.int32
+U8 = mybir.dt.uint8
+FP8X4 = mybir.dt.float8_e4m3fn_x4
+ALU = mybir.AluOpType
+ACT = mybir.ActivationFunctionType
+P = 128
+
+
+def tile_rows_lin_relu1_gate_kernel(tc, q, qa, ka, k, t, v, og, out):
+    nc = tc.nc
+    with ExitStack() as ctx:
+        sb = ctx.enter_context(tc.tile_pool(name="sb", bufs=1))
+        ps = ctx.enter_context(tc.psum_pool(name="ps", bufs=1))
+
+        def tl(name, shape, dtype):
+            return sb.tile(shape, dtype, name=name, align_bytes=64)
+
+        warm_in = tl("warm_in", [P, 1], F32)
+        warm_out = tl("warm_out", [P, 1], F32)
+        t_sb = tl("t_sb", [P, 4], F32)
+        qa_sb = tl("qa_sb", [P, 4], F32)
+        ka_sb = tl("ka_sb", [P, D], F32)
+        w = tl("w", [P, 4, 32, 4], F32)
+        k_raw = [tl("k_raw%d" % g, [P, 4, D], F32) for g in range(H)]
+        k_pos = [tl("k_pos%d" % g, [P, 4, 32, 4], F32) for g in range(H)]
+        k_bf = [tl("k_bf%d" % u, [P, 4, 2, 128], BF16) for u in range(2)]
+        k_codes = [tl("k_codes%d" % u, [P, 320], I32) for u in range(2)]
+        k_scales = [tl("k_scales%d" % u, [P, 320], U8) for u in range(2)]
+        k_wide = [tl("k_wide%d" % u, [P, 1152], I32) for u in range(2)]
+        v_raw = [tl("v_raw%d" % g, [P, 4, D], F32) for g in range(H)]
+        v_bf = [tl("v_bf%d" % g, [P, D, 4], BF16) for g in range(H)]
+        v_codes = [tl("v_codes%d" % g, [P, D], I32) for g in range(H)]
+        v_scales = [tl("v_scales%d" % g, [P, D], U8) for g in range(H)]
+        q_raw = [tl("q_raw%d" % c, [P, 4, 256], F32) for c in range(2)]
+        q_pos = [[tl("q_pos%d%d" % (c, a), [P, 2, 64, 4], F32) for a in range(2)] for c in range(2)]
+        q_bf = [tl("q_bf%d" % c, [P, 2, 128, 4], BF16) for c in range(2)]
+        q_codes = [tl("q_codes%d" % c, [P, 256], I32) for c in range(2)]
+        q_scales = [tl("q_scales%d" % c, [P, 256], U8) for c in range(2)]
+        s_bf = tl("s_bf", [P, D, 4], BF16)
+        s_codes = [tl("s_codes%d" % u, [P, D], I32) for u in range(2)]
+        s_scales = [tl("s_scales%d" % u, [P, D], U8) for u in range(2)]
+        og_raw = [[tl("og_raw%d%d" % (c, u), [P, 2, 256], F32) for u in range(2)] for c in range(2)]
+        gate = [[tl("gate%d%d" % (c, u), [P, 2, 256], F32) for u in range(2)] for c in range(2)]
+        y_sb = [[tl("y_sb%d%d" % (c, u), [P, 2, 256], F32) for u in range(2)] for c in range(2)]
+        s_ps = [ps.tile([P, 4, D], F32, name="s_ps%d" % u) for u in range(2)]
+        y_ps = [ps.tile([P, 2, 2, D], F32, name="y_ps%d" % g) for g in range(H)]
+
+        q_hbm = q.rearrange("h (p j) n -> (h p) j n", j=4)
+        og_hbm = og.rearrange("h (c s r) e -> s c h (r e)", c=2, r=2)
+        out_hbm = out.rearrange("h (c s r) e -> s c h (r e)", c=2, r=2)
+
+        def relu(eng, dst, src):
+            if eng == "A":
+                nc.scalar.activation(out=dst, in_=src, func=ACT.Relu)
+            elif eng == "G":
+                nc.gpsimd.tensor_scalar(out=dst, in0=src, scalar1=0.0, scalar2=0.0, op0=ALU.max, op1=ALU.add)
+            else:
+                nc.vector.tensor_scalar(out=dst, in0=src, scalar1=0.0, scalar2=None, op0=ALU.max)
+
+        def quant(codes, scales, src):
+            nc.vector.quantize_mx(out=codes.bitcast(FP8X4), scales=scales, in_=src)
+
+        def mm(dst, lc, ls, rc, rs, start, stop):
+            nc.tensor.matmul_mx(out=dst, lhsT=lc.bitcast(FP8X4), lhsT_scale=ls, rhs=rc.bitcast(FP8X4), rhs_scale=rs, start=start, stop=stop)
+
+        def load_k(g):
+            nc.sync.dma_start(out=k_raw[g][:], in_=k[g].rearrange("(p j) d -> p j d", j=4))
+
+        def load_v(g):
+            nc.sync.dma_start(out=v_raw[g][:], in_=v[g].rearrange("(p j) d -> p j d", j=4))
+
+        def load_q(c):
+            nc.sync.dma_start(out=q_raw[c][:], in_=q_hbm[:, :, 256 * c : 256 * c + 256])
+
+        def load_q_half(c, a):
+            nc.sync.dma_start(out=q_raw[c][:, :, 128 * a : 128 * a + 128], in_=q_hbm[:, :, 256 * c + 128 * a : 256 * c + 128 * a + 128])
+
+        def load_og(c, u):
+            nc.sync.dma_start(out=og_raw[c][u][:], in_=og_hbm[:, c, 2 * u : 2 * u + 2, :])
+
+        def load_t():
+            nc.sync.dma_start(out=t_sb[:], in_=t.rearrange("(p j) o -> p (j o)", j=4))
+
+        def load_ka():
+            nc.sync.dma_start(out=ka_sb[:], in_=ka)
+
+        def load_qa():
+            nc.sync.dma_start(out=qa_sb[:], in_=qa.rearrange("(p j) o -> p (j o)", j=4).unsqueeze(0).to_broadcast([H, 32, 4]))
+
+        def load_qa_head(g):
+            nc.sync.dma_start(out=qa_sb[32 * g : 32 * g + 32, :], in_=qa.rearrange("(p j) o -> p (j o)", j=4))
+
+        def make_w():
+            nc.vector.tensor_tensor(
+                out=w[:],
+                in0=ka_sb[:].rearrange("p (m j) -> p j m", j=4).unsqueeze(3).to_broadcast([P, 4, 32, 4]),
+                in1=t_sb[:].unsqueeze(1).unsqueeze(1).to_broadcast([P, 4, 32, 4]),
+                op=ALU.mult,
+            )
+
+        def k1(g, eng):
+            relu(eng, k_pos[g][:].rearrange("p j m x -> p m x j"), k_raw[g][:].rearrange("p x (m j) -> p m x j", j=4))
+
+        def k2(g):
+            nc.vector.scalar_tensor_tensor(
+                out=k_bf[g // 2][:, :, g % 2, :],
+                in0=k_pos[g][:].rearrange("p j m x -> p j (m x)"),
+                scalar=0.125,
+                in1=w[:].rearrange("p j m x -> p j (m x)"),
+                op0=ALU.add,
+                op1=ALU.mult,
+            )
+
+        def kq(u):
+            quant(k_codes[u][:, 64 * u : 64 * u + 256], k_scales[u][:, 64 * u : 64 * u + 256], k_bf[u][:].rearrange("p j h c -> p (j h c)"))
+
+        def kz(u):
+            dst = k_wide[u][:, 64 * u : 64 * u + 1088].rearrange("p (h x) -> p h x", h=2)[:, :, 0:512]
+            dst = dst.rearrange("p h (j y) -> p h j y", j=4)[:, :, :, 0:32]
+            src = k_codes[u][:, 64 * u : 64 * u + 256].rearrange("p (j h m) -> p h j m", j=4, h=2)
+            nc.vector.tensor_copy(out=dst, in_=src)
+
+        def vc(g, eng):
+            dst = v_bf[g][:].rearrange("p (c i) x -> p c x i", i=4)
+            src = v_raw[g][:].rearrange("p x (c i) -> p c x i", i=4)
+            if eng == "A":
+                nc.scalar.copy(out=dst, in_=src)
+            elif eng == "G":
+                nc.gpsimd.tensor_scalar(out=dst, in0=src, scalar1=1.0, scalar2=0.0, op0=ALU.mult, op1=ALU.add)
+            else:
+                nc.vector.tensor_copy(out=dst, in_=src)
+
+        def vq(g):
+            quant(v_codes[g][:], v_scales[g][:], v_bf[g][:].rearrange("p e x -> p (e x)"))
+
+        def m1_pair(u):
+            for j in range(4):
+                for h in range(2):
+                    g = 2 * u + h
+                    mm(s_ps[u][:, j, :], k_wide[u][:, 512 * h + 128 * j : 512 * h + 128 * j + 128], k_scales[u][:, 64 * j : 64 * j + 128],
+                       v_codes[g][:], v_scales[g][:], h == 0, h == 1)
+
+        def m1_head(g):
+            u = g // 2
+            for j in range(4):
+                mm(s_ps[g][:, j, :], k_codes[u][:, 64 * j : 64 * j + 128], k_scales[u][:, 64 * j : 64 * j + 128],
+                   v_codes[g][:], v_scales[g][:], True, True)
+
+        def evac(i, rows, eng):
+            dst = s_bf[rows * i : rows * i + rows, :, :]
+            src = s_ps[i][rows * i : rows * i + rows, :, :].rearrange("p j e -> p e j")
+            if eng == "A":
+                nc.scalar.activation(out=dst, in_=src, func=ACT.Copy, scale=1.0 / N)
+            else:
+                nc.vector.tensor_scalar(out=dst, in0=src, scalar1=1.0 / N, scalar2=None, op0=ALU.mult)
+
+        def sq(u):
+            rows = 64 * (u + 1)
+            quant(s_codes[u][0:rows, :], s_scales[u][0:rows, :], s_bf[0:rows, :, :].rearrange("p e j -> p (e j)"))
+
+        def q1(c, a, eng):
+            relu(eng, q_pos[c][a][:].rearrange("p r s j -> p s j r"),
+                 q_raw[c][:, :, 128 * a : 128 * a + 128].rearrange("p j (s r) -> p s j r", r=2))
+
+        def q2(c, a):
+            nc.vector.scalar_tensor_tensor(
+                out=q_bf[c][:, :, 64 * a : 64 * a + 64, :].rearrange("p r s j -> p r (s j)"),
+                in0=q_pos[c][a][:].rearrange("p r s j -> p (r s) j"),
+                scalar=0.125,
+                in1=qa_sb[:].unsqueeze(1).to_broadcast([P, 128, 4]),
+                op0=ALU.add,
+                op1=ALU.mult,
+            )
+
+        def qq(c):
+            quant(q_codes[c][:], q_scales[c][:], q_bf[c][:].rearrange("p r s j -> p (r s j)"))
+
+        def sig(c, u):
+            nc.scalar.activation(out=gate[c][u][:], in_=og_raw[c][u][:], func=ACT.Sigmoid)
+
+        def m2(c, g):
+            rows = slice(32 * g, 32 * g + 32)
+            u = g // 2
+            for r in range(2):
+                cols = slice(128 * r, 128 * r + 128)
+                mm(y_ps[g][:, c, r, :], q_codes[c][rows, cols], q_scales[c][rows, cols], s_codes[u][rows, :], s_scales[u][rows, :], True, True)
+
+        def yy(c, g):
+            nc.vector.tensor_tensor(
+                out=y_sb[c][g // 2][:, g % 2, :],
+                in0=y_ps[g][:, c, :, :].rearrange("p r e -> p (r e)"),
+                in1=gate[c][g // 2][:, g % 2, :],
+                op=ALU.mult,
+            )
+
+        def store(c, u):
+            nc.sync.dma_start(out=out_hbm[:, c, 2 * u : 2 * u + 2, :], in_=y_sb[c][u][:])
+
+        def store_head(c, g):
+            nc.sync.dma_start(out=out_hbm[:, c, g, :], in_=y_sb[c][g // 2][:, g % 2, :])
+
+        with tc.manual_schedule():
+            nc.vector.memset(warm_in[:], 0.0)
+            nc.scalar.activation(out=warm_out[:], in_=warm_in[:], func=ACT.Sigmoid)
+            for u in range(2):
+                nc.vector.memset(k_wide[u][:, 0:1024], 0)
+                nc.vector.memset(k_scales[u][:].bitcast(I32), 0)
+            load_k(0)
+            load_t()
+            load_ka()
+            load_k(3)
+            load_k(1)
+            k1(3, "A")
+            load_k(2)
+            k1(0, "V")
+            make_w()
+            load_v(1)
+            k1(1, "A")
+            load_v(0)
+            k1(2, "A")
+            k2(0)
+            k2(3)
+            k2(1)
+            k2(2)
+            kq(0)
+            vc(1, "A")
+            load_v(3)
+            kq(1)
+            kz(0)
+            load_q(0)
+            vc(0, "A")
+            load_v(2)
+            load_qa()
+            vq(0)
+            vq(1)
+            vc(3, "A")
+            q1(0, 1, "V")
+            q1(0, 0, "A")
+            load_q(1)
+            kz(1)
+            vq(3)
+            load_og(0, 1)
+            m1_pair(0)
+            q2(0, 1)
+            vc(2, "A")
+            vq(2)
+            q2(0, 0)
+            evac(0, 64, "A")
+            sq(0)
+            qq(0)
+            q1(1, 1, "A")
+            m1_pair(1)
+            load_og(0, 0)
+            q2(1, 1)
+            load_og(1, 0)
+            m2(0, 0)
+            q1(1, 0, "A")
+            q2(1, 0)
+            evac(1, 64, "A")
+            sq(1)
+            qq(1)
+            load_og(1, 1)
+            m2(0, 1)
+            sig(0, 0)
+            yy(0, 0)
+            sig(0, 1)
+            yy(0, 1)
+            m2(0, 2)
+            yy(0, 2)
+            m2(0, 3)
+            store(0, 0)
+            m2(1, 0)
+            yy(0, 3)
+            store(0, 1)
+            m2(1, 1)
+            sig(1, 0)
+            yy(1, 0)
+            m2(1, 2)
+            yy(1, 1)
+            sig(1, 1)
+            m2(1, 3)
+            store(1, 0)
+            yy(1, 2)
+            yy(1, 3)
+            store_head(1, 2)
+            store_head(1, 3)

@@ -51,7 +51,7 @@ def tile_rows_lin_relu1_gate_kernel(tc, q, qa, ka, k, t, v, og, out):
         og_raw = [[tl("og_raw%d%d" % (c, u), [P, 2, 256], F32) for u in range(2)] for c in range(2)]
         gate = [[tl("gate%d%d" % (c, u), [P, 2, 256], F32) for u in range(2)] for c in range(2)]
         y_sb = [[tl("y_sb%d%d" % (c, u), [P, 2, 256], F32) for u in range(2)] for c in range(2)]
-        s_ps = [ps.tile([P, 4, D], F32, name="s_ps%d" % u) for u in range(2)]
+        s_ps = [ps.tile([P, 4, D], F32, name="s_ps%d" % u) for u in range(4)]
         y_ps = [ps.tile([P, 2, 2, D], F32, name="y_ps%d" % g) for g in range(H)]
 
         q_hbm = q.rearrange("h (p j) n -> (h p) j n", j=4)
@@ -87,14 +87,14 @@ def tile_rows_lin_relu1_gate_kernel(tc, q, qa, ka, k, t, v, og, out):
         def load_og(c, u):
             nc.sync.dma_start(out=og_raw[c][u][:], in_=og_hbm[:, c, 2 * u : 2 * u + 2, :])
 
-        def load_t():
-            nc.sync.dma_start(out=t_sb[:], in_=t.rearrange("(p j) o -> p (j o)", j=4))
+        def load_t(eng):
+            eng.dma_start(out=t_sb[:], in_=t.rearrange("(p j) o -> p (j o)", j=4))
 
-        def load_ka():
-            nc.sync.dma_start(out=ka_sb[:], in_=ka)
+        def load_ka(eng):
+            eng.dma_start(out=ka_sb[:], in_=ka)
 
-        def load_qa():
-            nc.sync.dma_start(out=qa_sb[:], in_=qa.rearrange("(p j) o -> p (j o)", j=4).unsqueeze(0).to_broadcast([H, 32, 4]))
+        def load_qa(eng):
+            eng.dma_start(out=qa_sb[:], in_=qa.rearrange("(p j) o -> p (j o)", j=4).unsqueeze(0).to_broadcast([H, 32, 4]))
 
         def load_qa_head(g):
             nc.sync.dma_start(out=qa_sb[32 * g : 32 * g + 32, :], in_=qa.rearrange("(p j) o -> p (j o)", j=4))
@@ -146,7 +146,7 @@ def tile_rows_lin_relu1_gate_kernel(tc, q, qa, ka, k, t, v, og, out):
             for j in range(4):
                 for h in range(2):
                     g = 2 * u + h
-                    mm(s_ps[u][:, j, :], k_wide[u][:, 512 * h + 128 * j : 512 * h + 128 * j + 128], k_scales[u][:, 64 * j : 64 * j + 128],
+                    mm(s_ps[2 * u][:, j, :], k_wide[u][:, 512 * h + 128 * j : 512 * h + 128 * j + 128], k_scales[u][:, 64 * j : 64 * j + 128],
                        v_codes[g][:], v_scales[g][:], h == 0, h == 1)
 
         def m1_head(g):
@@ -155,9 +155,9 @@ def tile_rows_lin_relu1_gate_kernel(tc, q, qa, ka, k, t, v, og, out):
                 mm(s_ps[g][:, j, :], k_codes[u][:, 64 * j : 64 * j + 128], k_scales[u][:, 64 * j : 64 * j + 128],
                    v_codes[g][:], v_scales[g][:], True, True)
 
-        def evac(i, rows, eng):
+        def evac(b, i, rows, eng):
             dst = s_bf[rows * i : rows * i + rows, :, :]
-            src = s_ps[i][rows * i : rows * i + rows, :, :].rearrange("p j e -> p e j")
+            src = s_ps[b][rows * i : rows * i + rows, :, :].rearrange("p j e -> p e j")
             if eng == "A":
                 nc.scalar.activation(out=dst, in_=src, func=ACT.Copy, scale=1.0 / N)
             else:
@@ -210,85 +210,89 @@ def tile_rows_lin_relu1_gate_kernel(tc, q, qa, ka, k, t, v, og, out):
 
         with tc.manual_schedule():
             nc.vector.memset(warm_in[:], 0.0)
-            nc.scalar.activation(out=warm_out[:], in_=warm_in[:], func=ACT.Sigmoid)
             for u in range(2):
-                nc.vector.memset(k_wide[u][:, 0:1024], 0)
                 nc.vector.memset(k_scales[u][:].bitcast(I32), 0)
+            nc.vector.memset(k_wide[0][:, 0:1024], 0)
+            nc.gpsimd.memset(k_wide[1][:, 0:1024], 0)
+            load_t(nc.sync)
+            load_ka(nc.scalar)
             load_k(0)
-            load_t()
-            load_ka()
-            load_k(3)
+            nc.scalar.activation(out=warm_out[:], in_=warm_in[:], func=ACT.Sigmoid)
             load_k(1)
-            k1(3, "A")
             load_k(2)
-            k1(0, "V")
             make_w()
-            load_v(1)
+            load_k(3)
             k1(1, "A")
             load_v(0)
             k1(2, "A")
+            k1(0, "V")
+            load_v(1)
             k2(0)
-            k2(3)
-            k2(1)
-            k2(2)
-            kq(0)
-            vc(1, "A")
-            load_v(3)
-            kq(1)
-            kz(0)
+            k1(3, "A")
             load_q(0)
             vc(0, "A")
-            load_v(2)
-            load_qa()
+            k2(1)
+            k2(2)
+            k2(3)
+            kq(0)
             vq(0)
-            vq(1)
-            vc(3, "A")
-            q1(0, 1, "V")
-            q1(0, 0, "A")
-            load_q(1)
-            kz(1)
-            vq(3)
-            load_og(0, 1)
-            m1_pair(0)
-            q2(0, 1)
+            kq(1)
+            vc(1, "A")
+            q1(0, 1, "A")
+            load_v(2)
             vc(2, "A")
-            vq(2)
-            q2(0, 0)
-            evac(0, 64, "A")
-            sq(0)
-            qq(0)
-            q1(1, 1, "A")
-            m1_pair(1)
+            load_qa(nc.sync)
+            load_v(3)
+            vc(3, "A")
+            load_q(1)
+            kz(0)
+            vq(1)
+            m1_pair(0)
+            kz(1)
+            q1(0, 0, "V")
+            q2(0, 1)
             load_og(0, 0)
-            q2(1, 1)
+            evac(0, 0, 64, "A")
+            q2(0, 0)
+            load_og(0, 1)
+            vq(2)
+            vq(3)
+            q1(1, 1, "V")
+            qq(0)
+            m1_pair(1)
             load_og(1, 0)
-            m2(0, 0)
+            sq(0)
             q1(1, 0, "A")
-            q2(1, 0)
-            evac(1, 64, "A")
-            sq(1)
-            qq(1)
-            load_og(1, 1)
-            m2(0, 1)
+            q2(1, 1)
+            m2(0, 0)
             sig(0, 0)
+            q2(1, 0)
+            m2(0, 1)
             yy(0, 0)
-            sig(0, 1)
+            evac(2, 1, 64, "A")
+            sq(1)
             yy(0, 1)
             m2(0, 2)
-            yy(0, 2)
+            sig(0, 1)
+            qq(1)
             m2(0, 3)
-            store(0, 0)
+            yy(0, 2)
+            load_og(1, 1)
             m2(1, 0)
-            yy(0, 3)
-            store(0, 1)
-            m2(1, 1)
             sig(1, 0)
+            yy(0, 3)
+            store_head(0, 0)
+            m2(1, 1)
             yy(1, 0)
+            store_head(0, 1)
+            sig(1, 1)
             m2(1, 2)
             yy(1, 1)
-            sig(1, 1)
+            store_head(0, 2)
+            store_head(0, 3)
+            store_head(1, 0)
+            store_head(1, 1)
             m2(1, 3)
-            store(1, 0)
             yy(1, 2)
             yy(1, 3)
             store_head(1, 2)

@@ -213,87 +213,83 @@ def tile_rows_lin_relu1_gate_kernel(tc, q, qa, ka, k, t, v, og, out):
             for u in range(2):
                 nc.vector.memset(k_scales[u][:].bitcast(I32), 0)
             nc.vector.memset(k_wide[0][:, 0:1024], 0)
-            nc.gpsimd.memset(k_wide[1][:, 0:1024], 0)
-            load_t(nc.sync)
-            load_ka(nc.scalar)
-            load_k(0)
+            nc.vector.memset(k_wide[1][:, 0:1024], 0)
             nc.scalar.activation(out=warm_out[:], in_=warm_in[:], func=ACT.Sigmoid)
+            load_k(0)
+            load_t(nc.sync)
+            load_ka(nc.sync)
             load_k(1)
             load_k(2)
-            make_w()
             load_k(3)
-            k1(1, "A")
+            load_qa(nc.sync)
             load_v(0)
-            k1(2, "A")
-            k1(0, "V")
             load_v(1)
-            k2(0)
-            k1(3, "A")
             load_q(0)
+            load_v(2)
+            load_v(3)
+            load_q(1)
+            load_og(0, 0)
+            load_og(0, 1)
+            load_og(1, 0)
+            load_og(1, 1)
+            k1(0, "A")
+            k1(1, "A")
+            k1(2, "A")
+            k1(3, "A")
             vc(0, "A")
+            vc(1, "A")
+            q1(0, 1, "A")
+            vc(2, "A")
+            vc(3, "A")
+            make_w()
+            k2(0)
             k2(1)
             k2(2)
             k2(3)
             kq(0)
             vq(0)
             kq(1)
-            vc(1, "A")
-            q1(0, 1, "A")
-            load_v(2)
-            vc(2, "A")
-            load_qa(nc.sync)
-            load_v(3)
-            vc(3, "A")
-            load_q(1)
-            kz(0)
             vq(1)
-            m1_pair(0)
+            kz(0)
             kz(1)
             q1(0, 0, "V")
             q2(0, 1)
-            load_og(0, 0)
-            evac(0, 0, 64, "A")
             q2(0, 0)
-            load_og(0, 1)
             vq(2)
             vq(3)
-            q1(1, 1, "V")
             qq(0)
+            q1(1, 0, "V")
+            m1_pair(0)
             m1_pair(1)
-            load_og(1, 0)
+            evac(0, 0, 64, "A")
+            q1(1, 1, "A")
+            sig(0, 0)
+            evac(2, 1, 64, "A")
+            sig(0, 1)
+            sig(1, 0)
+            sig(1, 1)
             sq(0)
-            q1(1, 0, "A")
+            q2(1, 0)
             q2(1, 1)
             m2(0, 0)
-            sig(0, 0)
-            q2(1, 0)
             m2(0, 1)
             yy(0, 0)
-            evac(2, 1, 64, "A")
             sq(1)
             yy(0, 1)
-            m2(0, 2)
-            sig(0, 1)
             qq(1)
+            m2(0, 2)
             m2(0, 3)
-            yy(0, 2)
-            load_og(1, 1)
             m2(1, 0)
-            sig(1, 0)
-            yy(0, 3)
-            store_head(0, 0)
             m2(1, 1)
+            store(0, 0)
+            yy(0, 2)
+            yy(0, 3)
             yy(1, 0)
-            store_head(0, 1)
-            sig(1, 1)
-            m2(1, 2)
             yy(1, 1)
-            store_head(0, 2)
-            store_head(0, 3)
-            store_head(1, 0)
-            store_head(1, 1)
+            m2(1, 2)
             m2(1, 3)
+            store(0, 1)
+            store(1, 0)
             yy(1, 2)
             yy(1, 3)
-            store_head(1, 2)
-            store_head(1, 3)
+            store(1, 1)

from contextlib import ExitStack

import concourse.mybir as mybir

H, D, N = 4, 128, 512
FLOPS = 2 * 2 * H * N * D * D

F32 = mybir.dt.float32
BF16 = mybir.dt.bfloat16
I32 = mybir.dt.int32
U8 = mybir.dt.uint8
FP8X4 = mybir.dt.float8_e4m3fn_x4
ALU = mybir.AluOpType
ACT = mybir.ActivationFunctionType
P = 128


def tile_rows_lin_relu1_gate_kernel(tc, q, qa, ka, k, t, v, og, out):
    nc = tc.nc
    with ExitStack() as ctx:
        sb = ctx.enter_context(tc.tile_pool(name="sb", bufs=1))
        ps = ctx.enter_context(tc.psum_pool(name="ps", bufs=1))

        def tl(name, shape, dtype):
            return sb.tile(shape, dtype, name=name, align_bytes=64)

        warm_in = tl("warm_in", [P, 1], F32)
        warm_out = tl("warm_out", [P, 1], F32)
        t_sb = tl("t_sb", [P, 4], F32)
        qa_sb = tl("qa_sb", [P, 4], F32)
        ka_sb = tl("ka_sb", [P, D], F32)
        w = tl("w", [P, 4, 32, 4], F32)
        k_raw = [tl("k_raw%d" % g, [P, 4, D], F32) for g in range(H)]
        k_pos = [tl("k_pos%d" % g, [P, 4, 32, 4], F32) for g in range(H)]
        k_bf = [tl("k_bf%d" % u, [P, 4, 2, 128], BF16) for u in range(2)]
        k_codes = [tl("k_codes%d" % u, [P, 320], I32) for u in range(2)]
        k_scales = [tl("k_scales%d" % u, [P, 320], U8) for u in range(2)]
        k_wide = [tl("k_wide%d" % u, [P, 1152], I32) for u in range(2)]
        v_raw = [tl("v_raw%d" % g, [P, 4, D], F32) for g in range(H)]
        v_bf = [tl("v_bf%d" % g, [P, D, 4], BF16) for g in range(H)]
        v_codes = [tl("v_codes%d" % g, [P, D], I32) for g in range(H)]
        v_scales = [tl("v_scales%d" % g, [P, D], U8) for g in range(H)]
        q_raw = [tl("q_raw%d" % c, [P, 4, 256], F32) for c in range(2)]
        q_pos = [[tl("q_pos%d%d" % (c, a), [P, 2, 64, 4], F32) for a in range(2)] for c in range(2)]
        q_bf = [tl("q_bf%d" % c, [P, 2, 128, 4], BF16) for c in range(2)]
        q_codes = [tl("q_codes%d" % c, [P, 256], I32) for c in range(2)]
        q_scales = [tl("q_scales%d" % c, [P, 256], U8) for c in range(2)]
        s_bf = tl("s_bf", [P, D, 4], BF16)
        s_codes = [tl("s_codes%d" % u, [P, D], I32) for u in range(2)]
        s_scales = [tl("s_scales%d" % u, [P, D], U8) for u in range(2)]
        og_raw = [[tl("og_raw%d%d" % (c, u), [P, 2, 256], F32) for u in range(2)] for c in range(2)]
        gate = [[tl("gate%d%d" % (c, u), [P, 2, 256], F32) for u in range(2)] for c in range(2)]
        y_sb = [[tl("y_sb%d%d" % (c, u), [P, 2, 256], F32) for u in range(2)] for c in range(2)]
        s_ps = [ps.tile([P, 4, D], F32, name="s_ps%d" % u) for u in range(4)]
        y_ps = [ps.tile([P, 2, 2, D], F32, name="y_ps%d" % g) for g in range(H)]

        q_hbm = q.rearrange("h (p j) n -> (h p) j n", j=4)
        og_hbm = og.rearrange("h (c s r) e -> s c h (r e)", c=2, r=2)
        out_hbm = out.rearrange("h (c s r) e -> s c h (r e)", c=2, r=2)

        def relu(eng, dst, src):
            if eng == "A":
                nc.scalar.activation(out=dst, in_=src, func=ACT.Relu)
            elif eng == "G":
                nc.gpsimd.tensor_scalar(out=dst, in0=src, scalar1=0.0, scalar2=0.0, op0=ALU.max, op1=ALU.add)
            else:
                nc.vector.tensor_scalar(out=dst, in0=src, scalar1=0.0, scalar2=None, op0=ALU.max)

        def quant(codes, scales, src):
            nc.vector.quantize_mx(out=codes.bitcast(FP8X4), scales=scales, in_=src)

        def mm(dst, lc, ls, rc, rs, start, stop):
            nc.tensor.matmul_mx(out=dst, lhsT=lc.bitcast(FP8X4), lhsT_scale=ls, rhs=rc.bitcast(FP8X4), rhs_scale=rs, start=start, stop=stop)

        def load_k(g):
            nc.sync.dma_start(out=k_raw[g][:], in_=k[g].rearrange("(p j) d -> p j d", j=4))

        def load_v(g):
            nc.sync.dma_start(out=v_raw[g][:], in_=v[g].rearrange("(p j) d -> p j d", j=4))

        def load_q(c):
            nc.sync.dma_start(out=q_raw[c][:], in_=q_hbm[:, :, 256 * c : 256 * c + 256])

        def load_q_half(c, a):
            nc.sync.dma_start(out=q_raw[c][:, :, 128 * a : 128 * a + 128], in_=q_hbm[:, :, 256 * c + 128 * a : 256 * c + 128 * a + 128])

        def load_og(c, u):
            nc.sync.dma_start(out=og_raw[c][u][:], in_=og_hbm[:, c, 2 * u : 2 * u + 2, :])

        def load_t(eng):
            eng.dma_start(out=t_sb[:], in_=t.rearrange("(p j) o -> p (j o)", j=4))

        def load_ka(eng):
            eng.dma_start(out=ka_sb[:], in_=ka)

        def load_qa(eng):
            eng.dma_start(out=qa_sb[:], in_=qa.rearrange("(p j) o -> p (j o)", j=4).unsqueeze(0).to_broadcast([H, 32, 4]))

        def load_qa_head(g):
            nc.sync.dma_start(out=qa_sb[32 * g : 32 * g + 32, :], in_=qa.rearrange("(p j) o -> p (j o)", j=4))

        def make_w():
            nc.vector.tensor_tensor(
                out=w[:],
                in0=ka_sb[:].rearrange("p (m j) -> p j m", j=4).unsqueeze(3).to_broadcast([P, 4, 32, 4]),
                in1=t_sb[:].unsqueeze(1).unsqueeze(1).to_broadcast([P, 4, 32, 4]),
                op=ALU.mult,
            )

        def k1(g, eng):
            relu(eng, k_pos[g][:].rearrange("p j m x -> p m x j"), k_raw[g][:].rearrange("p x (m j) -> p m x j", j=4))

        def k2(g):
            nc.vector.scalar_tensor_tensor(
                out=k_bf[g // 2][:, :, g % 2, :],
                in0=k_pos[g][:].rearrange("p j m x -> p j (m x)"),
                scalar=0.125,
                in1=w[:].rearrange("p j m x -> p j (m x)"),
                op0=ALU.add,
                op1=ALU.mult,
            )

        def kq(u):
            quant(k_codes[u][:, 64 * u : 64 * u + 256], k_scales[u][:, 64 * u : 64 * u + 256], k_bf[u][:].rearrange("p j h c -> p (j h c)"))

        def kz(u):
            dst = k_wide[u][:, 64 * u : 64 * u + 1088].rearrange("p (h x) -> p h x", h=2)[:, :, 0:512]
            dst = dst.rearrange("p h (j y) -> p h j y", j=4)[:, :, :, 0:32]
            src = k_codes[u][:, 64 * u : 64 * u + 256].rearrange("p (j h m) -> p h j m", j=4, h=2)
            nc.vector.tensor_copy(out=dst, in_=src)

        def vc(g, eng):
            dst = v_bf[g][:].rearrange("p (c i) x -> p c x i", i=4)
            src = v_raw[g][:].rearrange("p x (c i) -> p c x i", i=4)
            if eng == "A":
                nc.scalar.copy(out=dst, in_=src)
            elif eng == "G":
                nc.gpsimd.tensor_scalar(out=dst, in0=src, scalar1=1.0, scalar2=0.0, op0=ALU.mult, op1=ALU.add)
            else:
                nc.vector.tensor_copy(out=dst, in_=src)

        def vq(g):
            quant(v_codes[g][:], v_scales[g][:], v_bf[g][:].rearrange("p e x -> p (e x)"))

        def m1_pair(u):
            for j in range(4):
                for h in range(2):
                    g = 2 * u + h
                    mm(s_ps[2 * u][:, j, :], k_wide[u][:, 512 * h + 128 * j : 512 * h + 128 * j + 128], k_scales[u][:, 64 * j : 64 * j + 128],
                       v_codes[g][:], v_scales[g][:], h == 0, h == 1)

        def m1_head(g):
            u = g // 2
            for j in range(4):
                mm(s_ps[g][:, j, :], k_codes[u][:, 64 * j : 64 * j + 128], k_scales[u][:, 64 * j : 64 * j + 128],
                   v_codes[g][:], v_scales[g][:], True, True)

        def evac(b, i, rows, eng):
            dst = s_bf[rows * i : rows * i + rows, :, :]
            src = s_ps[b][rows * i : rows * i + rows, :, :].rearrange("p j e -> p e j")
            if eng == "A":
                nc.scalar.activation(out=dst, in_=src, func=ACT.Copy, scale=1.0 / N)
            else:
                nc.vector.tensor_scalar(out=dst, in0=src, scalar1=1.0 / N, scalar2=None, op0=ALU.mult)

        def sq(u):
            rows = 64 * (u + 1)
            quant(s_codes[u][0:rows, :], s_scales[u][0:rows, :], s_bf[0:rows, :, :].rearrange("p e j -> p (e j)"))

        def q1(c, a, eng):
            relu(eng, q_pos[c][a][:].rearrange("p r s j -> p s j r"),
                 q_raw[c][:, :, 128 * a : 128 * a + 128].rearrange("p j (s r) -> p s j r", r=2))

        def q2(c, a):
            nc.vector.scalar_tensor_tensor(
                out=q_bf[c][:, :, 64 * a : 64 * a + 64, :].rearrange("p r s j -> p r (s j)"),
                in0=q_pos[c][a][:].rearrange("p r s j -> p (r s) j"),
                scalar=0.125,
                in1=qa_sb[:].unsqueeze(1).to_broadcast([P, 128, 4]),
                op0=ALU.add,
                op1=ALU.mult,
            )

        def qq(c):
            quant(q_codes[c][:], q_scales[c][:], q_bf[c][:].rearrange("p r s j -> p (r s j)"))

        def sig(c, u):
            nc.scalar.activation(out=gate[c][u][:], in_=og_raw[c][u][:], func=ACT.Sigmoid)

        def m2(c, g):
            rows = slice(32 * g, 32 * g + 32)
            u = g // 2
            for r in range(2):
                cols = slice(128 * r, 128 * r + 128)
                mm(y_ps[g][:, c, r, :], q_codes[c][rows, cols], q_scales[c][rows, cols], s_codes[u][rows, :], s_scales[u][rows, :], True, True)

        def yy(c, g):
            nc.vector.tensor_tensor(
                out=y_sb[c][g // 2][:, g % 2, :],
                in0=y_ps[g][:, c, :, :].rearrange("p r e -> p (r e)"),
                in1=gate[c][g // 2][:, g % 2, :],
                op=ALU.mult,
            )

        def store(c, u):
            nc.sync.dma_start(out=out_hbm[:, c, 2 * u : 2 * u + 2, :], in_=y_sb[c][u][:])

        def store_head(c, g):
            nc.sync.dma_start(out=out_hbm[:, c, g, :], in_=y_sb[c][g // 2][:, g % 2, :])

        with tc.manual_schedule():
            nc.vector.memset(warm_in[:], 0.0)
            for u in range(2):
                nc.vector.memset(k_scales[u][:].bitcast(I32), 0)
            nc.vector.memset(k_wide[0][:, 0:1024], 0)
            nc.vector.memset(k_wide[1][:, 0:1024], 0)
            nc.scalar.activation(out=warm_out[:], in_=warm_in[:], func=ACT.Sigmoid)
            load_k(0)
            load_t(nc.sync)
            load_ka(nc.sync)
            load_k(1)
            load_k(2)
            load_k(3)
            load_qa(nc.sync)
            load_v(0)
            load_v(1)
            load_q(0)
            load_v(2)
            load_v(3)
            load_q(1)
            load_og(0, 0)
            load_og(0, 1)
            load_og(1, 0)
            load_og(1, 1)
            k1(0, "A")
            k1(1, "A")
            k1(2, "A")
            k1(3, "A")
            vc(0, "A")
            vc(1, "A")
            q1(0, 1, "A")
            vc(2, "A")
            vc(3, "A")
            make_w()
            k2(0)
            k2(1)
            k2(2)
            k2(3)
            kq(0)
            vq(0)
            kq(1)
            vq(1)
            kz(0)
            kz(1)
            q1(0, 0, "V")
            q2(0, 1)
            q2(0, 0)
            vq(2)
            vq(3)
            qq(0)
            q1(1, 0, "V")
            m1_pair(0)
            m1_pair(1)
            evac(0, 0, 64, "A")
            q1(1, 1, "A")
            sig(0, 0)
            evac(2, 1, 64, "A")
            sig(0, 1)
            sig(1, 0)
            sig(1, 1)
            sq(0)
            q2(1, 0)
            q2(1, 1)
            m2(0, 0)
            m2(0, 1)
            yy(0, 0)
            sq(1)
            yy(0, 1)
            qq(1)
            m2(0, 2)
            m2(0, 3)
            m2(1, 0)
            m2(1, 1)
            store(0, 0)
            yy(0, 2)
            yy(0, 3)
            yy(1, 0)
            yy(1, 1)
            m2(1, 2)
            m2(1, 3)
            store(0, 1)
            store(1, 0)
            yy(1, 2)
            yy(1, 3)
            store(1, 1)
